import numpy as np
CORES = [0,1,2,3,4,5,6,7,8,9,10,11,12,13,14,15]
N = 16
COUNTS = [[0,2,3,4,5,0,1,2,3,4,0,6,1,2,3,0],[4,5,6,1,0,3,4,5,6,0,2,3,4,5,0,1],[1,2,3,0,5,6,1,2,0,4,5,6,1,0,3,4],[4,5,0,1,2,3,4,0,6,1,2,3,0,5,6,1],[1,0,3,4,5,6,0,2,3,4,5,0,1,2,3,4],[0,5,6,1,2,0,4,5,6,1,0,3,4,5,6,0],[1,2,3,4,0,6,1,2,3,0,5,6,1,2,0,4],[4,5,6,0,2,3,4,5,0,1,2,3,4,0,6,1],[1,2,0,4,5,6,1,0,3,4,5,6,0,2,3,4],[4,0,6,1,2,3,0,5,6,1,2,0,4,5,6,1],[0,2,3,4,5,0,1,2,3,4,0,6,1,2,3,0],[4,5,6,1,0,3,4,5,6,0,2,3,4,5,0,1],[1,2,3,0,5,6,1,2,0,4,5,6,1,0,3,4],[4,5,0,1,2,3,4,0,6,1,2,3,0,5,6,1],[1,0,3,4,5,6,0,2,3,4,5,0,1,2,3,4],[0,5,6,1,2,0,4,5,6,1,0,3,4,5,6,0]]
XW, YW = 49, 60
def setup_inputs(rng):
    return {"x": rng.standard_normal((N, 128, XW), dtype=np.float32)}
def reference(x):
    y = np.full((N, 128, YW), np.nan, x.dtype)
    fill = [0] * N
    for s in range(N):
        o = 0
        for d in range(N):
            c = COUNTS[s][d]
            y[d][:, fill[d]:fill[d] + c] = x[s][:, o:o + c]
            o += c; fill[d] += c
    return {"y": y}

@@ -1,0 +1,174 @@
+import concourse.bass as bass
+
+NENG = 16
+XENG = 8
+PIECES = None
+
+LANDW = 60 + 2 * 16
+SCRATCH = {
+    "xs": ("sbuf", [128, 49], "float32"),
+    "stage": ("sbuf", [128, 64], "float32"),
+    "land": ("sbuf", [128, LANDW], "float32"),
+}
+MARGIN = 16
+SEMAPHORES = ["ld", "plc", "own", "st", "stg", "arr", "sent"]
+
+
+def share_engines(kinds, total):
+    n = len(kinds)
+    e = 1
+    while 2 * e * n <= total:
+        e *= 2
+    cnt = [e] * n
+    spare = total - e * n
+    for want in (0, 1):
+        for i in range(n):
+            if kinds[i] == want and spare >= cnt[i] and cnt[i] == e:
+                spare -= cnt[i]
+                cnt[i] *= 2
+    return cnt
+
+
+def masks_for(cnt):
+    order = sorted(range(len(cnt)), key=lambda i: -cnt[i])
+    out = [0] * len(cnt)
+    pos = 0
+    for i in order:
+        out[i] = ((1 << cnt[i]) - 1) << pos
+        pos += cnt[i]
+    return out
+
+
+def split_width(c, pieces):
+    if pieces is None:
+        return [c]
+    return list(pieces[c])
+
+
+def make_plan(tables, cores, topo):
+    C = tables["COUNTS"]
+    n = len(cores)
+    R = range(n)
+    chip = [topo.chip(cores[r]) for r in R]
+    xoff = [[sum(C[s][:d]) for d in R] for s in R]
+    yoff = [[sum(C[q][d] for q in range(s)) for s in R] for d in R]
+    ytot = [sum(C[s][d] for s in R) for d in R]
+
+    lo, tot, front = [0] * n, [0] * n, [False] * n
+    for d in R:
+        far = [s for s in R if chip[s] != chip[d]]
+        assert far == list(range(far[0], far[-1] + 1)) and (far[0] == 0 or far[-1] == n - 1)
+        lo[d] = yoff[d][far[0]]
+        tot[d] = sum(C[s][d] for s in far)
+        front[d] = far[0] == 0
+
+    gate, stoff, serves, wide = [None] * n, [0] * n, {}, {}
+    for ch in sorted(set(chip)):
+        far = [d for d in R if chip[d] != ch]
+        for die in (0, 1):
+            gws = [s for s in R if chip[s] == ch and topo.die(cores[s]) == die
+                   and topo.may_write(cores[s], cores[far[0]])]
+            ds = sorted([d for d in far if topo.die(cores[d]) == die], key=lambda d: -tot[d])
+            per = len(ds) // len(gws)
+            for i, gw in enumerate(gws):
+                mine = ds[i * per:(i + 1) * per]
+                if not front[mine[0]]:
+                    mine = mine[::-1]
+                pos = 0
+                for d in mine:
+                    gate[d], stoff[d] = gw, pos
+                    pos += tot[d]
+                serves[gw] = mine
+                wide[gw] = max(tot[d] for d in mine)
+
+    prog = {}
+    for s in R:
+        local, items = [], []
+        for d in R:
+            c = C[s][d]
+            if c == 0:
+                continue
+            if d == s:
+                local.append(("own", "land", MARGIN + yoff[d][s], xoff[s][d], c))
+            elif chip[d] == chip[s]:
+                items.append((1, d, "land", MARGIN + yoff[d][s], xoff[s][d], c))
+            elif gate[d] == s:
+                local.append(("plc", "stage", stoff[d] + yoff[d][s] - lo[d], xoff[s][d], c))
+            else:
+                items.append((0, gate[d], "stage", stoff[d] + yoff[d][s] - lo[d], xoff[s][d], c))
+        bywidth = {}
+        for kind, dst, buf, dcol, scol, c in items:
+            part = 0
+            for w in split_width(c, PIECES if kind == 0 else None):
+                bywidth.setdefault(w, []).append((kind, dst, buf, dcol + part, scol + part, w))
+                part += w
+        calls = []
+        for w in sorted(bywidth, key=lambda w: (min(t[0] for t in bywidth[w]), -len(bywidth[w]), -w)):
+            ts = sorted(bywidth[w])
+            ms = masks_for(share_engines([t[0] for t in ts], NENG))
+            calls.append([(dst, buf, dcol, "xs", scol, w, m, "stg" if kind == 0 else "arr")
+                          for (kind, dst, buf, dcol, scol, w), m in zip(ts, ms)])
+        cross = []
+        if s in serves:
+            W = wide[s]
+            ms = masks_for(share_engines([0] * len(serves[s]), XENG))
+            for d, m in zip(serves[s], ms):
+                pad = W - tot[d]
+                assert pad <= MARGIN
+                if front[d]:
+                    cross.append((d, "land", MARGIN + lo[d] - pad, "stage", stoff[d] - pad, W, m, "arr"))
+                else:
+                    cross.append((d, "land", MARGIN + lo[d], "stage", stoff[d], W, m, "arr"))
+        prog[s] = {"local": local, "calls": calls, "cross": cross, "ytot": ytot[s]}
+
+    for s in R:
+        prog[s]["stg"] = prog[s]["arr"] = prog[s]["sent"] = 0
+    for s in R:
+        for call in prog[s]["calls"] + ([prog[s]["cross"]] if prog[s]["cross"] else []):
+            for (dst, buf, dcol, sbuf, scol, w, m, sem) in call:
+                e = bin(m).count("1")
+                prog[dst][sem] += e
+                prog[s]["sent"] += e
+    return prog
+
+
+def rank_program(g, core, T, topo):
+    rank = T.rank_of(core)
+    if rank is None:
+        return
+    me = make_plan(T.tables, T.cores, topo)[rank]
+    bufs = {"xs": T.xs, "stage": T.stage, "land": T.land}
+    sems = {"stg": T.sem.stg, "arr": T.sem.arr, "plc": T.sem.plc, "own": T.sem.own}
+
+    def fused(call):
+        trs = []
+        for (dst, buf, dcol, sbuf, scol, w, m, sem) in call:
+            rid, pid, se = topo.addr(T.cores[dst])
+            trs.append(bass.RemoteDMATransfer(
+                dst_ids=[bass.DstId(rid=rid, pnc=pid)], dma_engine_mask=m, remote_sem=sems[sem],
+                src=bufs[sbuf][:, scol:scol + w], dst=bufs[buf][:, dcol:dcol + w]))
+        g.remote_dma_fused(trs, local_sem=T.sem.sent)
+
+    g.dma_start(T.xs[:], T.x[:]).then_inc(T.sem.ld, 16)
+    done = {"plc": 0, "own": 0}
+    for (sem, buf, dcol, scol, c) in sorted(me["local"], key=lambda t: t[0] != "plc"):
+        g.dma_start(bufs[buf][:, dcol:dcol + c], T.x[:, scol:scol + c],
+                    allow_slow_non_contiguous=(c == 1)).then_inc(sems[sem], 16)
+        done[sem] += 16
+    g.wait_ge(T.sem.ld, 16)
+
+    for call in me["calls"]:
+        fused(call)
+
+    if me["cross"]:
+        g.wait_ge(T.sem.stg, me["stg"])
+        if done["plc"]:
+            g.wait_ge(T.sem.plc, done["plc"])
+        fused(me["cross"])
+
+    g.wait_ge(T.sem.arr, me["arr"])
+    if done["own"]:
+        g.wait_ge(T.sem.own, done["own"])
+    g.dma_start(T.y[:, 0:me["ytot"]], T.land[:, MARGIN:MARGIN + me["ytot"]]).then_inc(T.sem.st, 16)
+    g.wait_ge(T.sem.sent, me["sent"])
+    g.wait_ge(T.sem.st, 16)

@@ -2,7 +2,6 @@ import concourse.bass as bass
 
 NENG = 16
 XENG = 8
-PIECES = None
 
 LANDW = 60 + 2 * 16
 SCRATCH = {
@@ -37,12 +36,6 @@ def masks_for(cnt):
         out[i] = ((1 << cnt[i]) - 1) << pos
         pos += cnt[i]
     return out
-
-
-def split_width(c, pieces):
-    if pieces is None:
-        return [c]
-    return list(pieces[c])
 
 
 def make_plan(tables, cores, topo):
@@ -83,7 +76,8 @@ def make_plan(tables, cores, topo):
 
     prog = {}
     for s in R:
-        local, items = [], []
+        local = []
+        bywidth = {}
         for d in R:
             c = C[s][d]
             if c == 0:
@@ -91,23 +85,17 @@ def make_plan(tables, cores, topo):
             if d == s:
                 local.append(("own", "land", MARGIN + yoff[d][s], xoff[s][d], c))
             elif chip[d] == chip[s]:
-                items.append((1, d, "land", MARGIN + yoff[d][s], xoff[s][d], c))
+                bywidth.setdefault(c, []).append((1, d, "land", MARGIN + yoff[d][s], xoff[s][d]))
             elif gate[d] == s:
                 local.append(("plc", "stage", stoff[d] + yoff[d][s] - lo[d], xoff[s][d], c))
             else:
-                items.append((0, gate[d], "stage", stoff[d] + yoff[d][s] - lo[d], xoff[s][d], c))
-        bywidth = {}
-        for kind, dst, buf, dcol, scol, c in items:
-            part = 0
-            for w in split_width(c, PIECES if kind == 0 else None):
-                bywidth.setdefault(w, []).append((kind, dst, buf, dcol + part, scol + part, w))
-                part += w
+                bywidth.setdefault(c, []).append((0, gate[d], "stage", stoff[d] + yoff[d][s] - lo[d], xoff[s][d]))
         calls = []
         for w in sorted(bywidth, key=lambda w: (min(t[0] for t in bywidth[w]), -len(bywidth[w]), -w)):
             ts = sorted(bywidth[w])
             ms = masks_for(share_engines([t[0] for t in ts], NENG))
-            calls.append([(dst, buf, dcol, "xs", scol, w, m, "stg" if kind == 0 else "arr")
-                          for (kind, dst, buf, dcol, scol, w), m in zip(ts, ms)])
+            calls.append([(dst, buf, dcol, "xs", scol, w, m, "arr" if kind else "stg")
+                          for (kind, dst, buf, dcol, scol), m in zip(ts, ms)])
         cross = []
         if s in serves:
             W = wide[s]
@@ -139,6 +127,7 @@ def rank_program(g, core, T, topo):
     me = make_plan(T.tables, T.cores, topo)[rank]
     bufs = {"xs": T.xs, "stage": T.stage, "land": T.land}
     sems = {"stg": T.sem.stg, "arr": T.sem.arr, "plc": T.sem.plc, "own": T.sem.own}
+    done = {"plc": 0, "own": 0}
 
     def fused(call):
         trs = []
@@ -149,12 +138,15 @@ def rank_program(g, core, T, topo):
                 src=bufs[sbuf][:, scol:scol + w], dst=bufs[buf][:, dcol:dcol + w]))
         g.remote_dma_fused(trs, local_sem=T.sem.sent)
 
+    def place(which):
+        for (sem, buf, dcol, scol, c) in me["local"]:
+            if sem == which:
+                g.dma_start(bufs[buf][:, dcol:dcol + c], T.x[:, scol:scol + c],
+                            allow_slow_non_contiguous=(c == 1)).then_inc(sems[sem], 16)
+                done[sem] += 16
+
     g.dma_start(T.xs[:], T.x[:]).then_inc(T.sem.ld, 16)
-    done = {"plc": 0, "own": 0}
-    for (sem, buf, dcol, scol, c) in sorted(me["local"], key=lambda t: t[0] != "plc"):
-        g.dma_start(bufs[buf][:, dcol:dcol + c], T.x[:, scol:scol + c],
-                    allow_slow_non_contiguous=(c == 1)).then_inc(sems[sem], 16)
-        done[sem] += 16
+    place("plc")
     g.wait_ge(T.sem.ld, 16)
 
     for call in me["calls"]:
@@ -165,6 +157,8 @@ def rank_program(g, core, T, topo):
         if done["plc"]:
             g.wait_ge(T.sem.plc, done["plc"])
         fused(me["cross"])
+
+    place("own")
 
     g.wait_ge(T.sem.arr, me["arr"])
     if done["own"]:

@@ -38,6 +38,18 @@ def masks_for(cnt):
     return out
 
 
+def deals(k, ds):
+    if k == 0:
+        return [[]]
+    out = []
+    for i in range(len(ds)):
+        for j in range(i + 1, len(ds)):
+            rest = ds[:i] + ds[i + 1:j] + ds[j + 1:]
+            for tail in deals(k - 1, rest):
+                out.append([(ds[i], ds[j])] + tail)
+    return out
+
+
 def make_plan(tables, cores, topo):
     C = tables["COUNTS"]
     n = len(cores)
@@ -58,21 +70,27 @@ def make_plan(tables, cores, topo):
     gate, stoff, serves, wide = [None] * n, [0] * n, {}, {}
     for ch in sorted(set(chip)):
         far = [d for d in R if chip[d] != ch]
-        for die in (0, 1):
-            gws = [s for s in R if chip[s] == ch and topo.die(cores[s]) == die
-                   and topo.may_write(cores[s], cores[far[0]])]
-            ds = sorted([d for d in far if topo.die(cores[d]) == die], key=lambda d: -tot[d])
-            per = len(ds) // len(gws)
-            for i, gw in enumerate(gws):
-                mine = ds[i * per:(i + 1) * per]
-                if not front[mine[0]]:
-                    mine = mine[::-1]
-                pos = 0
-                for d in mine:
-                    gate[d], stoff[d] = gw, pos
-                    pos += tot[d]
-                serves[gw] = mine
-                wide[gw] = max(tot[d] for d in mine)
+        gws = [s for s in R if chip[s] == ch and topo.may_write(cores[s], cores[far[0]])]
+        assert len(far) == 2 * len(gws)
+
+        def cost(deal):
+            copies = [sum(1 for d in pr if C[gw][d]) for gw, pr in zip(gws, deal)]
+            off = sum(1 for gw, pr in zip(gws, deal) for d in pr
+                      if topo.die(cores[d]) != topo.die(cores[gw]))
+            pad = sum(abs(tot[a] - tot[b]) for a, b in deal)
+            return (max(copies), sum(copies), off, pad)
+
+        best = min(deals(len(gws), far), key=cost)
+        for gw, pr in zip(gws, best):
+            mine = sorted(pr, key=lambda d: -tot[d])
+            if not front[mine[0]]:
+                mine = mine[::-1]
+            pos = 0
+            for d in mine:
+                gate[d], stoff[d] = gw, pos
+                pos += tot[d]
+            serves[gw] = mine
+            wide[gw] = max(tot[d] for d in mine)
 
     prog = {}
     for s in R:

import concourse.bass as bass

NENG = 16
XENG = 8

LANDW = 60 + 2 * 16
SCRATCH = {
    "xs": ("sbuf", [128, 49], "float32"),
    "stage": ("sbuf", [128, 64], "float32"),
    "land": ("sbuf", [128, LANDW], "float32"),
}
MARGIN = 16
SEMAPHORES = ["ld", "plc", "own", "st", "stg", "arr", "sent"]


def share_engines(kinds, total):
    n = len(kinds)
    e = 1
    while 2 * e * n <= total:
        e *= 2
    cnt = [e] * n
    spare = total - e * n
    for want in (0, 1):
        for i in range(n):
            if kinds[i] == want and spare >= cnt[i] and cnt[i] == e:
                spare -= cnt[i]
                cnt[i] *= 2
    return cnt


def masks_for(cnt):
    order = sorted(range(len(cnt)), key=lambda i: -cnt[i])
    out = [0] * len(cnt)
    pos = 0
    for i in order:
        out[i] = ((1 << cnt[i]) - 1) << pos
        pos += cnt[i]
    return out


def deals(k, ds):
    if k == 0:
        return [[]]
    out = []
    for i in range(len(ds)):
        for j in range(i + 1, len(ds)):
            rest = ds[:i] + ds[i + 1:j] + ds[j + 1:]
            for tail in deals(k - 1, rest):
                out.append([(ds[i], ds[j])] + tail)
    return out


def make_plan(tables, cores, topo):
    C = tables["COUNTS"]
    n = len(cores)
    R = range(n)
    chip = [topo.chip(cores[r]) for r in R]
    xoff = [[sum(C[s][:d]) for d in R] for s in R]
    yoff = [[sum(C[q][d] for q in range(s)) for s in R] for d in R]
    ytot = [sum(C[s][d] for s in R) for d in R]

    lo, tot, front = [0] * n, [0] * n, [False] * n
    for d in R:
        far = [s for s in R if chip[s] != chip[d]]
        assert far == list(range(far[0], far[-1] + 1)) and (far[0] == 0 or far[-1] == n - 1)
        lo[d] = yoff[d][far[0]]
        tot[d] = sum(C[s][d] for s in far)
        front[d] = far[0] == 0

    gate, stoff, serves, wide = [None] * n, [0] * n, {}, {}
    for ch in sorted(set(chip)):
        far = [d for d in R if chip[d] != ch]
        gws = [s for s in R if chip[s] == ch and topo.may_write(cores[s], cores[far[0]])]
        assert len(far) == 2 * len(gws)

        def cost(deal):
            copies = [sum(1 for d in pr if C[gw][d]) for gw, pr in zip(gws, deal)]
            off = sum(1 for gw, pr in zip(gws, deal) for d in pr
                      if topo.die(cores[d]) != topo.die(cores[gw]))
            pad = sum(abs(tot[a] - tot[b]) for a, b in deal)
            return (max(copies), sum(copies), off, pad)

        best = min(deals(len(gws), far), key=cost)
        for gw, pr in zip(gws, best):
            mine = sorted(pr, key=lambda d: -tot[d])
            if not front[mine[0]]:
                mine = mine[::-1]
            pos = 0
            for d in mine:
                gate[d], stoff[d] = gw, pos
                pos += tot[d]
            serves[gw] = mine
            wide[gw] = max(tot[d] for d in mine)

    prog = {}
    for s in R:
        local = []
        bywidth = {}
        for d in R:
            c = C[s][d]
            if c == 0:
                continue
            if d == s:
                local.append(("own", "land", MARGIN + yoff[d][s], xoff[s][d], c))
            elif chip[d] == chip[s]:
                bywidth.setdefault(c, []).append((1, d, "land", MARGIN + yoff[d][s], xoff[s][d]))
            elif gate[d] == s:
                local.append(("plc", "stage", stoff[d] + yoff[d][s] - lo[d], xoff[s][d], c))
            else:
                bywidth.setdefault(c, []).append((0, gate[d], "stage", stoff[d] + yoff[d][s] - lo[d], xoff[s][d]))
        calls = []
        for w in sorted(bywidth, key=lambda w: (min(t[0] for t in bywidth[w]), -len(bywidth[w]), -w)):
            ts = sorted(bywidth[w])
            ms = masks_for(share_engines([t[0] for t in ts], NENG))
            calls.append([(dst, buf, dcol, "xs", scol, w, m, "arr" if kind else "stg")
                          for (kind, dst, buf, dcol, scol), m in zip(ts, ms)])
        cross = []
        if s in serves:
            W = wide[s]
            ms = masks_for(share_engines([0] * len(serves[s]), XENG))
            for d, m in zip(serves[s], ms):
                pad = W - tot[d]
                assert pad <= MARGIN
                if front[d]:
                    cross.append((d, "land", MARGIN + lo[d] - pad, "stage", stoff[d] - pad, W, m, "arr"))
                else:
                    cross.append((d, "land", MARGIN + lo[d], "stage", stoff[d], W, m, "arr"))
        prog[s] = {"local": local, "calls": calls, "cross": cross, "ytot": ytot[s]}

    for s in R:
        prog[s]["stg"] = prog[s]["arr"] = prog[s]["sent"] = 0
    for s in R:
        for call in prog[s]["calls"] + ([prog[s]["cross"]] if prog[s]["cross"] else []):
            for (dst, buf, dcol, sbuf, scol, w, m, sem) in call:
                e = bin(m).count("1")
                prog[dst][sem] += e
                prog[s]["sent"] += e
    return prog


def rank_program(g, core, T, topo):
    rank = T.rank_of(core)
    if rank is None:
        return
    me = make_plan(T.tables, T.cores, topo)[rank]
    bufs = {"xs": T.xs, "stage": T.stage, "land": T.land}
    sems = {"stg": T.sem.stg, "arr": T.sem.arr, "plc": T.sem.plc, "own": T.sem.own}
    done = {"plc": 0, "own": 0}

    def fused(call):
        trs = []
        for (dst, buf, dcol, sbuf, scol, w, m, sem) in call:
            rid, pid, se = topo.addr(T.cores[dst])
            trs.append(bass.RemoteDMATransfer(
                dst_ids=[bass.DstId(rid=rid, pnc=pid)], dma_engine_mask=m, remote_sem=sems[sem],
                src=bufs[sbuf][:, scol:scol + w], dst=bufs[buf][:, dcol:dcol + w]))
        g.remote_dma_fused(trs, local_sem=T.sem.sent)

    def place(which):
        for (sem, buf, dcol, scol, c) in me["local"]:
            if sem == which:
                g.dma_start(bufs[buf][:, dcol:dcol + c], T.x[:, scol:scol + c],
                            allow_slow_non_contiguous=(c == 1)).then_inc(sems[sem], 16)
                done[sem] += 16

    g.dma_start(T.xs[:], T.x[:]).then_inc(T.sem.ld, 16)
    place("plc")
    g.wait_ge(T.sem.ld, 16)

    for call in me["calls"]:
        fused(call)

    if me["cross"]:
        g.wait_ge(T.sem.stg, me["stg"])
        if done["plc"]:
            g.wait_ge(T.sem.plc, done["plc"])
        fused(me["cross"])

    place("own")

    g.wait_ge(T.sem.arr, me["arr"])
    if done["own"]:
        g.wait_ge(T.sem.own, done["own"])
    g.dma_start(T.y[:, 0:me["ytot"]], T.land[:, MARGIN:MARGIN + me["ytot"]]).then_inc(T.sem.st, 16)
    g.wait_ge(T.sem.sent, me["sent"])
    g.wait_ge(T.sem.st, 16)
